import numpy as np
import ml_dtypes


def mxq(x, axis, fmt="e4m3"):
    dtype, down = {"e4m3": (ml_dtypes.float8_e4m3fn, 7), "e5m2": (ml_dtypes.float8_e5m2, 14)}[fmt]
    v = np.moveaxis(np.asarray(x, np.float32).astype(ml_dtypes.bfloat16).astype(np.float64), axis, -1)
    blocks = v.reshape(v.shape[:-1] + (-1, 32))
    amax = np.abs(blocks).max(-1, keepdims=True)
    byte = np.maximum(np.where(amax > 0, np.frexp(amax)[1] - 1 + 127, 0) - down, 1)
    scale = np.exp2(byte - 127.0)
    codes = (blocks / scale).astype(np.float32).astype(dtype).astype(np.float64)
    return np.moveaxis((codes * scale).reshape(v.shape), -1, axis)


WIDE = False


def mx_kscale(k):
    if not WIDE:
        return np.ones(k)
    levels = np.array([10, -10, 5, -5, 0])
    if k % 512:
        return np.exp2(np.random.permutation(np.resize(levels, k // 32))).repeat(32)
    a = np.empty((k // 512, 16))
    for p in range(k // 512):
        a[p, :8] = np.random.permutation(np.resize(levels, 8))
        for g in range(8):
            far = levels[np.abs(levels - a[p, g]) >= 10]
            a[p, g + 8] = far[np.random.randint(len(far))]
    return np.exp2(a.ravel()).repeat(32)


def f64(x):
    return np.asarray(x).astype(np.float64)


def striped(idx):
    return np.tile(np.asarray(idx).reshape(-1, 16).T, (8, 1)).astype(np.uint16)


def unstriped(offs):
    return offs[:16].T.reshape(-1).astype(np.int64)


E2M1 = np.array([0.0, 0.5, 1.0, 1.5, 2.0, 3.0, 4.0, 6.0, -0.0, -0.5, -1.0, -1.5, -2.0, -3.0, -4.0, -6.0])


def pack_weight(w, fmt):
    k, n = w.shape
    w = f64(np.asarray(w, np.float32).astype(ml_dtypes.bfloat16)).reshape(k // 32, 32, n)
    amax = np.abs(w).max(1)
    if fmt == "e4m3":
        byte = np.frexp(amax)[1] - 1 + 127 - 7
    else:
        mant, ex = np.frexp(amax / 6.0)
        byte = np.where(mant > 0.5, ex, ex - 1) + 127
    byte = np.clip(np.where(amax > 0, byte, 1), 1, 254)
    scaled = (w * np.exp2(127.0 - byte)[:, None, :]).reshape(k, n).astype(np.float32)
    by_word = np.ascontiguousarray(scaled.reshape(k // 512, 128, 4, n).transpose(0, 1, 3, 2))
    if fmt == "e4m3":
        words = by_word.astype(ml_dtypes.float8_e4m3fn).view(np.uint8)
    else:
        c = by_word.astype(ml_dtypes.float4_e2m1fn).view(np.uint8) & 0xF
        words = (c[..., 0::2] | (c[..., 1::2] << 4)).reshape(k // 512, 128, 2 * n)
    return np.ascontiguousarray(words), np.ascontiguousarray(byte.astype(np.uint8).reshape(k // 512, 16, n))


def unpack_weight(words, scales, fmt):
    g, _, n = scales.shape
    words = np.ascontiguousarray(words).reshape(g, 128, n, -1)
    if fmt == "e4m3":
        vals = words.view(ml_dtypes.float8_e4m3fn).astype(np.float64)
    else:
        nib = np.empty((g, 128, n, 4), np.uint8)
        nib[..., 0::2] = words & 0xF
        nib[..., 1::2] = words >> 4
        vals = E2M1[nib]
    vals = vals * np.repeat(np.exp2(scales.astype(np.float64) - 127.0), 8, axis=1)[..., None]
    return vals.transpose(0, 1, 3, 2).reshape(g * 512, n)


B, N, T, D, DV, NQ = 1, 1024, 2048, 512, 256, 128
PAGE = 64
DRAFT = 128


def setup_inputs():
    n = np.random.standard_normal
    pages = np.random.permutation(T // PAGE)[:B * N // PAGE]
    idx = (pages[:, None] * PAGE + np.arange(PAGE)[None, :]).reshape(-1)
    s = mx_kscale(D)[:, None]
    u = np.ones(T)
    u[idx] = mx_kscale(B * N)
    r = np.random.uniform(0.5, 2.0, T)
    k = n((D, T)) / s
    v = n((DV, T)) / (u * r)
    kp = pack_weight(k, "e4m3")
    when = np.zeros(T)
    when[idx] = np.concatenate([np.concatenate([np.arange(N - DRAFT), N - DRAFT + np.random.randint(0, 16, DRAFT)]) for b in range(B)])
    return {
        "qT": (n((B, D, NQ)) * s * (1.00 / np.sqrt(D))).astype(np.float32),
        "k_words": kp[0],
        "k_scales": kp[1],
        "vT": v.astype(np.float32),
        "vs": np.tile(u * r, (128, 1)).astype(np.float32),
        "pos": np.tile(when, (128, 1)).astype(np.float32),
        "qpos": np.random.randint(N - DRAFT, N - DRAFT + 16, (B, NQ, 1)).astype(np.float32),
        "offs": striped(idx),
    }


def reference(qT, k_words, k_scales, vT, vs, pos, qpos, offs):
    idx = unstriped(offs)
    k = unpack_weight(k_words, k_scales, "e4m3")
    v = f64(vT)
    pick = lambda x: x[:, idx].reshape(x.shape[0], B, N).transpose(1, 0, 2)
    q = f64(qT)
    score = mxq(q, 1, "e4m3").transpose(0, 2, 1) @ pick(k)
    score = np.where(pick(f64(pos))[:, :1, :] <= f64(qpos), score, -30000.0)
    m = score.max(-1, keepdims=True)
    p = np.exp(score - m)
    total = p.sum(-1, keepdims=True)
    w = p * pick(f64(vs))[:, :1, :]
    y = mxq(w, 2, "e4m3") @ mxq(pick(v).transpose(0, 2, 1), 1, "e4m3")
    y = y / total
    return y

@@ -1,0 +1,207 @@
+from contextlib import ExitStack
+
+import concourse.mybir as mybir
+from concourse.masks import make_identity
+
+F32 = mybir.dt.float32
+BF16 = mybir.dt.bfloat16
+I32 = mybir.dt.int32
+U32 = mybir.dt.uint32
+U16 = mybir.dt.uint16
+U8 = mybir.dt.uint8
+FP8X4 = mybir.dt.float8_e4m3fn_x4
+ALU = mybir.AluOpType
+ACT = mybir.ActivationFunctionType
+
+P = 128
+NQ, N, T, D, DV = 128, 1024, 2048, 512, 256
+PACK = 4
+KP = P * PACK
+PASSES = N // KP
+BLOCKS = KP // 32
+RUN = 8
+COLS = KP // 16
+V_CHUNKS = 4
+V_CHUNK = T // V_CHUNKS
+PLACE_SCALE = 2.0 ** 100
+MASKED = 2.0 ** 80
+ROW = P - 1
+
+FLOPS = 2 * NQ * N * (D + DV)
+
+
+def tile_attend_draft_kernel(tc, qT, k_words, k_scales, vT, vs, pos, qpos, offs, out):
+    nc = tc.nc
+    with ExitStack() as ctx:
+        sb = ctx.enter_context(tc.tile_pool(name="sb", bufs=1))
+        ps = ctx.enter_context(tc.psum_pool(name="ps", bufs=1))
+
+        def sbuf(name, shape, dtype, tag=""):
+            return sb.tile(shape, dtype, name=name, tag=tag or name, align_bytes=64)
+
+        def bank(name, tag, shape):
+            return ps.tile(shape, F32, name=name, tag=tag)
+
+        offsets = sbuf("offsets", [P, N // 16], U16)
+        ks_pool = sbuf("ks_pool", [P, T], U8)
+        vs_pool = sbuf("vs_pool", [P, T], F32)
+        pos_pool = sbuf("pos_pool", [P, T], F32)
+        kw_pool = sbuf("kw_pool", [P, T], I32)
+        q_raw = sbuf("q_raw", [P, PACK, NQ], F32)
+        q_place = sbuf("q_place", [P, 1], F32)
+        v_raw = [sbuf(f"v_raw{c}", [P, 2, V_CHUNK], F32) for c in range(V_CHUNKS)]
+        v_pool = sbuf("v_pool", [P, T, 2], BF16)
+        ident = sbuf("ident", [P, P], F32)
+        warm = sbuf("warm", [P, 1], F32)
+        warm_out = sbuf("warm_out", [P, 1], F32)
+
+        nc.vector.memset(ks_pool[:].bitcast(I32), 0)
+        nc.vector.memset(vs_pool[0:ROW, :], 0.0)
+        nc.gpsimd.memset(warm[:], 0.0)
+        nc.scalar.activation(out=warm_out[:], in_=warm[:], func=ACT.Exp)
+        make_identity(nc, ident[:])
+
+        nc.sync.dma_start(offsets[:], offs)
+        nc.sync.dma_start(out=vs_pool[ROW:P, :], in_=vs[ROW:P, :])
+        nc.sync.dma_start(out=pos_pool[:], in_=pos)
+        for quad in range(4):
+            nc.sync.dma_start(
+                out=ks_pool[32 * quad : 32 * quad + 4, :].bitcast(I32),
+                in_=k_scales[0, 4 * quad : 4 * quad + 4, :].bitcast(I32),
+            )
+        nc.sync.dma_start(out=q_raw[:], in_=qT[0].rearrange("(p j) w -> p j w", j=PACK))
+        nc.sync.dma_start(out=kw_pool[:], in_=k_words[0].rearrange("p t r -> p (t r)").bitcast(I32))
+        nc.sync.dma_start(out=q_place[:], in_=qpos[0])
+        v_pairs = vT.rearrange("(p j) t -> p j t", j=2)
+        for c in range(V_CHUNKS):
+            nc.sync.dma_start(out=v_raw[c][:], in_=v_pairs[:, :, c * V_CHUNK : (c + 1) * V_CHUNK])
+
+        def listed(g):
+            return offsets[:, g * COLS : (g + 1) * COLS]
+
+        vs_dealt = sbuf("vs_dealt", [P, PACK, PASSES * BLOCKS, RUN], U32)
+        nc.vector.tensor_copy(
+            out=vs_dealt[:].rearrange("p t b j -> p b t j"),
+            in_=vs_pool[:].bitcast(U32).indirect(offsets[:]),
+        )
+        vs_turned = []
+        for g in range(PASSES):
+            turned = bank(f"vs_turned{g}", f"vs{g}", [P, PACK, P])
+            for t in range(PACK):
+                src = vs_dealt[:, t, g * BLOCKS : (g + 1) * BLOCKS, :].rearrange("p b j -> p (b j)").bitcast(F32)
+                nc.tensor.transpose(turned[:, t, :], src, ident[:])
+            vs_turned.append(turned)
+
+        pos_g = sbuf("pos_g", [P, N], F32)
+        nc.vector.tensor_copy(out=pos_g[:], in_=pos_pool[:].indirect(offsets[:]))
+        q_bias = sbuf("q_bias", [P, 1], F32)
+        nc.gpsimd.tensor_scalar(out=q_bias[:], in0=q_place[:], scalar1=-PLACE_SCALE, scalar2=0.0, op0=ALU.mult, op1=ALU.add)
+        ahead = sbuf("ahead", [P, N], F32)
+        nc.scalar.activation(out=ahead[:], in_=pos_g[:], func=ACT.Relu, bias=q_bias[:], scale=PLACE_SCALE)
+
+        q_bf = sbuf("q_bf", [P, NQ, PACK], BF16)
+        nc.scalar.copy(out=q_bf[:], in_=q_raw[:].rearrange("p j w -> p w j"))
+        q_codes = sbuf("q_codes", [P, NQ], U32)
+        q_scales = sbuf("q_scales", [P, NQ], U8)
+        nc.vector.quantize_mx(out=q_codes[:].bitcast(FP8X4), scales=q_scales[:], in_=q_bf[:].rearrange("p w j -> p (w j)"))
+
+        ks_g = sbuf("ks_g", [P, N], U8)
+        nc.vector.tensor_copy(out=ks_g[:], in_=ks_pool[:].indirect(offsets[:]))
+        neg = sbuf("neg", [P, N], F32)
+        kw_g = [sbuf(f"kw_g{g}", [P, KP], U32) for g in range(PASSES)]
+        scores = [bank(f"scores{g}", f"sc{g}", [P, KP]) for g in range(PASSES)]
+        for g in range(PASSES):
+            nc.vector.tensor_copy(out=kw_g[g][:], in_=kw_pool[:].bitcast(U32).indirect(listed(g)))
+            nc.tensor.matmul_mx(
+                out=scores[g][:],
+                lhsT=q_codes[:].bitcast(FP8X4),
+                lhsT_scale=q_scales[:],
+                rhs=kw_g[g][:].bitcast(FP8X4),
+                rhs_scale=ks_g[:, g * KP : (g + 1) * KP],
+                start=True,
+                stop=True,
+            )
+        for g in range(PASSES):
+            cols = slice(g * KP, (g + 1) * KP)
+            nc.vector.scalar_tensor_tensor(
+                out=neg[:, cols], in0=ahead[:, cols], scalar=MASKED, in1=scores[g][:], op0=ALU.min, op1=ALU.subtract
+            )
+        neg_max = sbuf("neg_max", [P, 1], F32)
+        nc.vector.tensor_reduce(out=neg_max[:], in_=neg[:], axis=mybir.AxisListType.X, op=ALU.min)
+
+        for c in range(V_CHUNKS):
+            nc.scalar.activation(
+                out=v_pool[:, c * V_CHUNK : (c + 1) * V_CHUNK, :], in_=v_raw[c][:].rearrange("p j t -> p t j"), func=ACT.Copy
+            )
+
+        part_sum = [sbuf(f"part_sum{g}", [P, 1], F32) for g in range(PASSES)]
+        p_turned = []
+        for g in range(PASSES):
+            p_dealt = sbuf(f"p_dealt{g}", [P, PACK, BLOCKS, RUN], F32, tag=f"v_raw{V_CHUNKS - 1 - g}")
+            nc.scalar.activation(
+                out=p_dealt[:],
+                in_=neg[:, g * KP : (g + 1) * KP].rearrange("p (b t j) -> p t b j", t=PACK, j=RUN),
+                func=ACT.Exp,
+                bias=neg_max[:],
+                scale=-1.0,
+                accum_out=part_sum[g][:],
+            )
+            turned = bank(f"p_turned{g}", f"sc{g}", [P, PACK, NQ])
+            for t in range(PACK):
+                nc.tensor.transpose(turned[:, t, :], p_dealt[:, t, :, :].rearrange("p b j -> p (b j)"), ident[:])
+            p_turned.append(turned)
+        vs_col = [neg[:, g * KP : g * KP + PACK] for g in range(PASSES)]
+        for g in range(PASSES):
+            nc.scalar.copy(out=vs_col[g], in_=vs_turned[g][:, :, ROW])
+
+        v_words = v_pool[:].rearrange("p t j -> p (t j)").bitcast(U32)
+        v_bf = []
+        for g in range(PASSES):
+            v_dealt = sbuf(f"v_dealt{g}", [P, PACK, BLOCKS, RUN], U32)
+            nc.vector.tensor_copy(out=v_dealt[:].rearrange("p t b j -> p b t j"), in_=v_words.indirect(listed(g)))
+            turned = bank(f"v_turned{g}", f"vs{g}", [P, PACK, P])
+            for t in range(PACK):
+                nc.tensor.transpose(turned[:, t, :], v_dealt[:, t, :, :].rearrange("p b j -> p (b j)").bitcast(F32), ident[:])
+            woven = sbuf(f"v_bf{g}", [P, DV, PACK], BF16)
+            nc.scalar.copy(out=woven[:], in_=turned[:].bitcast(BF16).rearrange("p t e -> p e t"))
+            v_bf.append(woven)
+
+        w_codes, w_scales = [], []
+        w_bf = []
+        for g in range(PASSES):
+            woven = sbuf(f"w_bf{g}", [P, NQ, PACK], BF16)
+            nc.vector.tensor_tensor(
+                out=woven[:],
+                in0=p_turned[g][:].rearrange("p t q -> p q t"),
+                in1=vs_col[g].unsqueeze(1).to_broadcast([P, NQ, PACK]),
+                op=ALU.mult,
+            )
+            w_bf.append(woven)
+        for g in range(PASSES):
+            codes = sbuf(f"w_codes{g}", [P, NQ], U32)
+            scales = sbuf(f"w_scales{g}", [P, NQ], U8)
+            nc.vector.quantize_mx(out=codes[:].bitcast(FP8X4), scales=scales[:], in_=w_bf[g][:].rearrange("p q t -> p (q t)"))
+            w_codes.append(codes)
+            w_scales.append(scales)
+        total = sbuf("total", [P, 1], F32)
+        nc.gpsimd.tensor_tensor(out=total[:], in0=part_sum[0][:], in1=part_sum[1][:], op=ALU.add)
+        inv_total = sbuf("inv_total", [P, 1], F32)
+        nc.vector.reciprocal(out=inv_total[:], in_=total[:])
+
+        acc = bank("acc", "acc", [P, DV])
+        for g in range(PASSES):
+            codes = sbuf(f"v_codes{g}", [P, DV], U32)
+            scales = sbuf(f"v_scales{g}", [P, DV], U8)
+            nc.vector.quantize_mx(out=codes[:].bitcast(FP8X4), scales=scales[:], in_=v_bf[g][:].rearrange("p e t -> p (e t)"))
+            nc.tensor.matmul_mx(
+                out=acc[:],
+                lhsT=w_codes[g][:].bitcast(FP8X4),
+                lhsT_scale=w_scales[g][:],
+                rhs=codes[:].bitcast(FP8X4),
+                rhs_scale=scales[:],
+                start=(g == 0),
+                stop=(g == PASSES - 1),
+            )
+        result = sbuf("result", [P, DV], F32)
+        nc.vector.tensor_scalar(out=result[:], in0=acc[:], scalar1=inv_total[:], scalar2=None, op0=ALU.mult)
+        nc.sync.dma_start(out=out[0], in_=result[:])

@@ -19,7 +19,8 @@ PACK = 4
 KP = P * PACK
 PASSES = N // KP
 BLOCKS = KP // 32
-RUN = 8
+HALF = 16
+TILES = KP // P
 COLS = KP // 16
 V_CHUNKS = 4
 V_CHUNK = T // V_CHUNKS
@@ -50,54 +51,60 @@ def tile_attend_draft_kernel(tc, qT, k_words, k_scales, vT, vs, pos, qpos, offs,
         q_raw = sbuf("q_raw", [P, PACK, NQ], F32)
         q_place = sbuf("q_place", [P, 1], F32)
         v_raw = [sbuf(f"v_raw{c}", [P, 2, V_CHUNK], F32) for c in range(V_CHUNKS)]
-        v_pool = sbuf("v_pool", [P, T, 2], BF16)
         ident = sbuf("ident", [P, P], F32)
         warm = sbuf("warm", [P, 1], F32)
         warm_out = sbuf("warm_out", [P, 1], F32)
 
         nc.vector.memset(ks_pool[:].bitcast(I32), 0)
-        nc.vector.memset(vs_pool[0:ROW, :], 0.0)
-        nc.gpsimd.memset(warm[:], 0.0)
-        nc.scalar.activation(out=warm_out[:], in_=warm[:], func=ACT.Exp)
-        make_identity(nc, ident[:])
-
+        nc.gpsimd.memset(pos_pool[0:ROW, :], 0.0)
         nc.sync.dma_start(offsets[:], offs)
-        nc.sync.dma_start(out=vs_pool[ROW:P, :], in_=vs[ROW:P, :])
-        nc.sync.dma_start(out=pos_pool[:], in_=pos)
+        nc.sync.dma_start(out=pos_pool[ROW:P, :], in_=pos[ROW:P, :])
         for quad in range(4):
-            nc.sync.dma_start(
+            nc.scalar.dma_start(
                 out=ks_pool[32 * quad : 32 * quad + 4, :].bitcast(I32),
                 in_=k_scales[0, 4 * quad : 4 * quad + 4, :].bitcast(I32),
             )
+        nc.vector.memset(warm[:], 0.0)
+        nc.scalar.activation(out=warm_out[:], in_=warm[:], func=ACT.Exp)
+        make_identity(nc, ident[:])
+
+        v_pairs = vT.rearrange("(p j) t -> p j t", j=2)
+
+        def load_values(c):
+            nc.sync.dma_start(out=v_raw[c][:], in_=v_pairs[:, :, c * V_CHUNK : (c + 1) * V_CHUNK])
+
+        nc.sync.dma_start(out=q_place[:], in_=qpos[0])
         nc.sync.dma_start(out=q_raw[:], in_=qT[0].rearrange("(p j) w -> p j w", j=PACK))
         nc.sync.dma_start(out=kw_pool[:], in_=k_words[0].rearrange("p t r -> p (t r)").bitcast(I32))
-        nc.sync.dma_start(out=q_place[:], in_=qpos[0])
-        v_pairs = vT.rearrange("(p j) t -> p j t", j=2)
-        for c in range(V_CHUNKS):
-            nc.sync.dma_start(out=v_raw[c][:], in_=v_pairs[:, :, c * V_CHUNK : (c + 1) * V_CHUNK])
+        for c in range(V_CHUNKS - 1):
+            load_values(c)
+        nc.sync.dma_start(out=vs_pool[:], in_=vs)
+        load_values(V_CHUNKS - 1)
 
         def listed(g):
             return offsets[:, g * COLS : (g + 1) * COLS]
 
-        vs_dealt = sbuf("vs_dealt", [P, PACK, PASSES * BLOCKS, RUN], U32)
-        nc.vector.tensor_copy(
-            out=vs_dealt[:].rearrange("p t b j -> p b t j"),
-            in_=vs_pool[:].bitcast(U32).indirect(offsets[:]),
-        )
-        vs_turned = []
-        for g in range(PASSES):
-            turned = bank(f"vs_turned{g}", f"vs{g}", [P, PACK, P])
-            for t in range(PACK):
-                src = vs_dealt[:, t, g * BLOCKS : (g + 1) * BLOCKS, :].rearrange("p b j -> p (b j)").bitcast(F32)
-                nc.tensor.transpose(turned[:, t, :], src, ident[:])
-            vs_turned.append(turned)
-
-        pos_g = sbuf("pos_g", [P, N], F32)
-        nc.vector.tensor_copy(out=pos_g[:], in_=pos_pool[:].indirect(offsets[:]))
-        q_bias = sbuf("q_bias", [P, 1], F32)
+        q_bias = sbuf("q_bias", [P, 1], F32, tag="v_pool")
         nc.gpsimd.tensor_scalar(out=q_bias[:], in0=q_place[:], scalar1=-PLACE_SCALE, scalar2=0.0, op0=ALU.mult, op1=ALU.add)
         ahead = sbuf("ahead", [P, N], F32)
-        nc.scalar.activation(out=ahead[:], in_=pos_g[:], func=ACT.Relu, bias=q_bias[:], scale=PLACE_SCALE)
+        pos_g = [sbuf(f"pos_g{g}", [P, KP], F32) for g in range(PASSES)]
+        for g in range(PASSES):
+            nc.vector.tensor_copy(out=pos_g[g][:], in_=pos_pool[:].indirect(listed(g)))
+        pos_col = []
+        for g in range(PASSES):
+            turned = bank(f"pos_turned{g}", f"pt{g}", [P, TILES, P])
+            for c in range(TILES):
+                nc.tensor.transpose(turned[:, c, :], pos_g[g][:, c * P : (c + 1) * P], ident[:])
+            col = sbuf(f"pos_col{g}", [P, TILES], F32)
+            nc.scalar.copy(out=col[:], in_=turned[:, :, ROW])
+            pos_col.append(col)
+        for g in range(PASSES):
+            spread = bank(f"pos_spread{g}", f"pb{g}", [P, KP])
+            for c in range(TILES):
+                nc.tensor.transpose(spread[:, c * P : (c + 1) * P], pos_col[g][:, c : c + 1].to_broadcast([P, P]), ident[:])
+            nc.scalar.activation(
+                out=ahead[:, g * KP : (g + 1) * KP], in_=spread[:], func=ACT.Relu, bias=q_bias[:], scale=PLACE_SCALE
+            )
 
         q_bf = sbuf("q_bf", [P, NQ, PACK], BF16)
         nc.scalar.copy(out=q_bf[:], in_=q_raw[:].rearrange("p j w -> p w j"))
@@ -105,11 +112,11 @@ def tile_attend_draft_kernel(tc, qT, k_words, k_scales, vT, vs, pos, qpos, offs,
         q_scales = sbuf("q_scales", [P, NQ], U8)
         nc.vector.quantize_mx(out=q_codes[:].bitcast(FP8X4), scales=q_scales[:], in_=q_bf[:].rearrange("p w j -> p (w j)"))
 
-        ks_g = sbuf("ks_g", [P, N], U8)
+        ks_g = sbuf("ks_g", [P, N], U8, tag="pos_g0")
         nc.vector.tensor_copy(out=ks_g[:], in_=ks_pool[:].indirect(offsets[:]))
         neg = sbuf("neg", [P, N], F32)
-        kw_g = [sbuf(f"kw_g{g}", [P, KP], U32) for g in range(PASSES)]
-        scores = [bank(f"scores{g}", f"sc{g}", [P, KP]) for g in range(PASSES)]
+        kw_g = [sbuf("kw_g0", [P, KP], U32, tag="pos_g1"), sbuf("kw_g1", [P, KP], U32)]
+        scores = [bank(f"scores{g}", f"pt{PASSES - 1 - g}", [P, KP]) for g in range(PASSES)]
         for g in range(PASSES):
             nc.vector.tensor_copy(out=kw_g[g][:], in_=kw_pool[:].bitcast(U32).indirect(listed(g)))
             nc.tensor.matmul_mx(
@@ -126,55 +133,66 @@ def tile_attend_draft_kernel(tc, qT, k_words, k_scales, vT, vs, pos, qpos, offs,
             nc.vector.scalar_tensor_tensor(
                 out=neg[:, cols], in0=ahead[:, cols], scalar=MASKED, in1=scores[g][:], op0=ALU.min, op1=ALU.subtract
             )
-        neg_max = sbuf("neg_max", [P, 1], F32)
+        neg_max = sbuf("neg_max", [P, 1], F32, tag=f"v_raw{V_CHUNKS - 2}")
         nc.vector.tensor_reduce(out=neg_max[:], in_=neg[:], axis=mybir.AxisListType.X, op=ALU.min)
 
+        v_pool = sbuf("v_pool", [P, T, 2], BF16)
         for c in range(V_CHUNKS):
             nc.scalar.activation(
                 out=v_pool[:, c * V_CHUNK : (c + 1) * V_CHUNK, :], in_=v_raw[c][:].rearrange("p j t -> p t j"), func=ACT.Copy
             )
 
+        vs_g = sbuf("vs_g", [P, N], F32)
+        nc.vector.tensor_copy(out=vs_g[:], in_=vs_pool[:].indirect(offsets[:]))
+
         part_sum = [sbuf(f"part_sum{g}", [P, 1], F32) for g in range(PASSES)]
-        p_turned = []
+        probs = []
         for g in range(PASSES):
-            p_dealt = sbuf(f"p_dealt{g}", [P, PACK, BLOCKS, RUN], F32, tag=f"v_raw{V_CHUNKS - 1 - g}")
+            prob = sbuf(f"prob{g}", [P, KP], F32, tag=f"v_raw{V_CHUNKS - 1}" if g == 0 else "")
             nc.scalar.activation(
-                out=p_dealt[:],
-                in_=neg[:, g * KP : (g + 1) * KP].rearrange("p (b t j) -> p t b j", t=PACK, j=RUN),
+                out=prob[:],
+                in_=neg[:, g * KP : (g + 1) * KP],
                 func=ACT.Exp,
                 bias=neg_max[:],
                 scale=-1.0,
                 accum_out=part_sum[g][:],
             )
-            turned = bank(f"p_turned{g}", f"sc{g}", [P, PACK, NQ])
-            for t in range(PACK):
-                nc.tensor.transpose(turned[:, t, :], p_dealt[:, t, :, :].rearrange("p b j -> p (b j)"), ident[:])
-            p_turned.append(turned)
-        vs_col = [neg[:, g * KP : g * KP + PACK] for g in range(PASSES)]
-        for g in range(PASSES):
-            nc.scalar.copy(out=vs_col[g], in_=vs_turned[g][:, :, ROW])
+            probs.append(prob)
 
         v_words = v_pool[:].rearrange("p t j -> p (t j)").bitcast(U32)
         v_bf = []
         for g in range(PASSES):
-            v_dealt = sbuf(f"v_dealt{g}", [P, PACK, BLOCKS, RUN], U32)
-            nc.vector.tensor_copy(out=v_dealt[:].rearrange("p t b j -> p b t j"), in_=v_words.indirect(listed(g)))
-            turned = bank(f"v_turned{g}", f"vs{g}", [P, PACK, P])
-            for t in range(PACK):
-                nc.tensor.transpose(turned[:, t, :], v_dealt[:, t, :, :].rearrange("p b j -> p (b j)").bitcast(F32), ident[:])
+            v_dealt = sbuf(f"v_dealt{g}", [P, 2, BLOCKS, HALF], U32)
+            nc.vector.tensor_copy(out=v_dealt[:].rearrange("p u b k -> p b u k"), in_=v_words.indirect(listed(g)))
+            turned = bank(f"v_turned{g}", f"pt{g}", [P, PACK, P])
+            for u in range(2):
+                half = v_dealt[:, u, :, :].rearrange("p b k -> p (b k)").bitcast(F32)
+                for e in range(2):
+                    nc.tensor.transpose(turned[:, 2 * u + e, :], half[:, e : 2 * P : 2], ident[:])
             woven = sbuf(f"v_bf{g}", [P, DV, PACK], BF16)
             nc.scalar.copy(out=woven[:], in_=turned[:].bitcast(BF16).rearrange("p t e -> p e t"))
             v_bf.append(woven)
 
         w_codes, w_scales = [], []
+        w_dealt = []
+        for g in range(PASSES):
+            dealt = sbuf(f"w_dealt{g}", [P, 2, BLOCKS, HALF], BF16)
+            nc.vector.tensor_tensor(
+                out=dealt[:].rearrange("p u b k -> p b u k"),
+                in0=probs[g][:].rearrange("p (b u k) -> p b u k", u=2, k=HALF),
+                in1=vs_g[:, g * KP : (g + 1) * KP].rearrange("p (b u k) -> p b u k", u=2, k=HALF),
+                op=ALU.mult,
+            )
+            w_dealt.append(dealt)
         w_bf = []
         for g in range(PASSES):
+            turned = bank(f"w_turned{g}", f"pt{g}", [P, 2, NQ])
+            for u in range(2):
+                nc.tensor.transpose(turned[:, u, :], w_dealt[g][:, u, :, :].rearrange("p b k -> p (b k)").bitcast(F32), ident[:])
             woven = sbuf(f"w_bf{g}", [P, NQ, PACK], BF16)
-            nc.vector.tensor_tensor(
-                out=woven[:],
-                in0=p_turned[g][:].rearrange("p t q -> p q t"),
-                in1=vs_col[g].unsqueeze(1).to_broadcast([P, NQ, PACK]),
-                op=ALU.mult,
+            nc.scalar.copy(
+                out=woven[:].rearrange("p q t -> p (q t)").bitcast(F32).rearrange("p (q u) -> p q u", u=2),
+                in_=turned[:].rearrange("p u q -> p q u"),
             )
             w_bf.append(woven)
         for g in range(PASSES):

@@ -76,10 +76,9 @@ def tile_attend_draft_kernel(tc, qT, k_words, k_scales, vT, vs, pos, qpos, offs,
         nc.sync.dma_start(out=q_place[:], in_=qpos[0])
         nc.sync.dma_start(out=q_raw[:], in_=qT[0].rearrange("(p j) w -> p j w", j=PACK))
         nc.sync.dma_start(out=kw_pool[:], in_=k_words[0].rearrange("p t r -> p (t r)").bitcast(I32))
-        for c in range(V_CHUNKS - 1):
+        for c in range(V_CHUNKS):
             load_values(c)
         nc.sync.dma_start(out=vs_pool[:], in_=vs)
-        load_values(V_CHUNKS - 1)
 
         def listed(g):
             return offsets[:, g * COLS : (g + 1) * COLS]
@@ -112,10 +111,10 @@ def tile_attend_draft_kernel(tc, qT, k_words, k_scales, vT, vs, pos, qpos, offs,
         q_scales = sbuf("q_scales", [P, NQ], U8)
         nc.vector.quantize_mx(out=q_codes[:].bitcast(FP8X4), scales=q_scales[:], in_=q_bf[:].rearrange("p w j -> p (w j)"))
 
-        ks_g = sbuf("ks_g", [P, N], U8, tag="pos_g0")
+        ks_g = sbuf("ks_g", [P, N], U8, tag="pos_pool")
         nc.vector.tensor_copy(out=ks_g[:], in_=ks_pool[:].indirect(offsets[:]))
         neg = sbuf("neg", [P, N], F32)
-        kw_g = [sbuf("kw_g0", [P, KP], U32, tag="pos_g1"), sbuf("kw_g1", [P, KP], U32)]
+        kw_g = [sbuf("kw_g0", [P, KP], U32, tag="ks_pool"), sbuf("kw_g1", [P, KP], U32)]
         scores = [bank(f"scores{g}", f"pt{PASSES - 1 - g}", [P, KP]) for g in range(PASSES)]
         for g in range(PASSES):
             nc.vector.tensor_copy(out=kw_g[g][:], in_=kw_pool[:].bitcast(U32).indirect(listed(g)))
@@ -133,7 +132,7 @@ def tile_attend_draft_kernel(tc, qT, k_words, k_scales, vT, vs, pos, qpos, offs,
             nc.vector.scalar_tensor_tensor(
                 out=neg[:, cols], in0=ahead[:, cols], scalar=MASKED, in1=scores[g][:], op0=ALU.min, op1=ALU.subtract
             )
-        neg_max = sbuf("neg_max", [P, 1], F32, tag=f"v_raw{V_CHUNKS - 2}")
+        neg_max = sbuf("neg_max", [P, 1], F32)
         nc.vector.tensor_reduce(out=neg_max[:], in_=neg[:], axis=mybir.AxisListType.X, op=ALU.min)
 
         v_pool = sbuf("v_pool", [P, T, 2], BF16)
@@ -142,8 +141,6 @@ def tile_attend_draft_kernel(tc, qT, k_words, k_scales, vT, vs, pos, qpos, offs,
                 out=v_pool[:, c * V_CHUNK : (c + 1) * V_CHUNK, :], in_=v_raw[c][:].rearrange("p j t -> p t j"), func=ACT.Copy
             )
 
-        vs_g = sbuf("vs_g", [P, N], F32)
-        nc.vector.tensor_copy(out=vs_g[:], in_=vs_pool[:].indirect(offsets[:]))
 
         part_sum = [sbuf(f"part_sum{g}", [P, 1], F32) for g in range(PASSES)]
         probs = []
@@ -162,7 +159,7 @@ def tile_attend_draft_kernel(tc, qT, k_words, k_scales, vT, vs, pos, qpos, offs,
         v_words = v_pool[:].rearrange("p t j -> p (t j)").bitcast(U32)
         v_bf = []
         for g in range(PASSES):
-            v_dealt = sbuf(f"v_dealt{g}", [P, 2, BLOCKS, HALF], U32)
+            v_dealt = sbuf(f"v_dealt{g}", [P, 2, BLOCKS, HALF], U32, tag="ahead" if g == 0 else "")
             nc.vector.tensor_copy(out=v_dealt[:].rearrange("p u b k -> p b u k"), in_=v_words.indirect(listed(g)))
             turned = bank(f"v_turned{g}", f"pt{g}", [P, PACK, P])
             for u in range(2):
@@ -173,6 +170,8 @@ def tile_attend_draft_kernel(tc, qT, k_words, k_scales, vT, vs, pos, qpos, offs,
             nc.scalar.copy(out=woven[:], in_=turned[:].bitcast(BF16).rearrange("p t e -> p e t"))
             v_bf.append(woven)
 
+        vs_g = sbuf("vs_g", [P, N], F32, tag="v_pool")
+        nc.vector.tensor_copy(out=vs_g[:], in_=vs_pool[:].indirect(offsets[:]))
         w_codes, w_scales = [], []
         w_dealt = []
         for g in range(PASSES):

from contextlib import ExitStack

import concourse.mybir as mybir
from concourse.masks import make_identity

F32 = mybir.dt.float32
BF16 = mybir.dt.bfloat16
I32 = mybir.dt.int32
U32 = mybir.dt.uint32
U16 = mybir.dt.uint16
U8 = mybir.dt.uint8
FP8X4 = mybir.dt.float8_e4m3fn_x4
ALU = mybir.AluOpType
ACT = mybir.ActivationFunctionType

P = 128
NQ, N, T, D, DV = 128, 1024, 2048, 512, 256
PACK = 4
KP = P * PACK
PASSES = N // KP
BLOCKS = KP // 32
HALF = 16
TILES = KP // P
COLS = KP // 16
V_CHUNKS = 4
V_CHUNK = T // V_CHUNKS
PLACE_SCALE = 2.0 ** 100
MASKED = 2.0 ** 80
ROW = P - 1

FLOPS = 2 * NQ * N * (D + DV)


def tile_attend_draft_kernel(tc, qT, k_words, k_scales, vT, vs, pos, qpos, offs, out):
    nc = tc.nc
    with ExitStack() as ctx:
        sb = ctx.enter_context(tc.tile_pool(name="sb", bufs=1))
        ps = ctx.enter_context(tc.psum_pool(name="ps", bufs=1))

        def sbuf(name, shape, dtype, tag=""):
            return sb.tile(shape, dtype, name=name, tag=tag or name, align_bytes=64)

        def bank(name, tag, shape):
            return ps.tile(shape, F32, name=name, tag=tag)

        offsets = sbuf("offsets", [P, N // 16], U16)
        ks_pool = sbuf("ks_pool", [P, T], U8)
        vs_pool = sbuf("vs_pool", [P, T], F32)
        pos_pool = sbuf("pos_pool", [P, T], F32)
        kw_pool = sbuf("kw_pool", [P, T], I32)
        q_raw = sbuf("q_raw", [P, PACK, NQ], F32)
        q_place = sbuf("q_place", [P, 1], F32)
        v_raw = [sbuf(f"v_raw{c}", [P, 2, V_CHUNK], F32) for c in range(V_CHUNKS)]
        ident = sbuf("ident", [P, P], F32)
        warm = sbuf("warm", [P, 1], F32)
        warm_out = sbuf("warm_out", [P, 1], F32)

        nc.vector.memset(ks_pool[:].bitcast(I32), 0)
        nc.gpsimd.memset(pos_pool[0:ROW, :], 0.0)
        nc.sync.dma_start(offsets[:], offs)
        nc.sync.dma_start(out=pos_pool[ROW:P, :], in_=pos[ROW:P, :])
        for quad in range(4):
            nc.scalar.dma_start(
                out=ks_pool[32 * quad : 32 * quad + 4, :].bitcast(I32),
                in_=k_scales[0, 4 * quad : 4 * quad + 4, :].bitcast(I32),
            )
        nc.vector.memset(warm[:], 0.0)
        nc.scalar.activation(out=warm_out[:], in_=warm[:], func=ACT.Exp)
        make_identity(nc, ident[:])

        v_pairs = vT.rearrange("(p j) t -> p j t", j=2)

        def load_values(c):
            nc.sync.dma_start(out=v_raw[c][:], in_=v_pairs[:, :, c * V_CHUNK : (c + 1) * V_CHUNK])

        nc.sync.dma_start(out=q_place[:], in_=qpos[0])
        nc.sync.dma_start(out=q_raw[:], in_=qT[0].rearrange("(p j) w -> p j w", j=PACK))
        nc.sync.dma_start(out=kw_pool[:], in_=k_words[0].rearrange("p t r -> p (t r)").bitcast(I32))
        for c in range(V_CHUNKS):
            load_values(c)
        nc.sync.dma_start(out=vs_pool[:], in_=vs)

        def listed(g):
            return offsets[:, g * COLS : (g + 1) * COLS]

        q_bias = sbuf("q_bias", [P, 1], F32, tag="v_pool")
        nc.gpsimd.tensor_scalar(out=q_bias[:], in0=q_place[:], scalar1=-PLACE_SCALE, scalar2=0.0, op0=ALU.mult, op1=ALU.add)
        ahead = sbuf("ahead", [P, N], F32)
        pos_g = [sbuf(f"pos_g{g}", [P, KP], F32) for g in range(PASSES)]
        for g in range(PASSES):
            nc.vector.tensor_copy(out=pos_g[g][:], in_=pos_pool[:].indirect(listed(g)))
        pos_col = []
        for g in range(PASSES):
            turned = bank(f"pos_turned{g}", f"pt{g}", [P, TILES, P])
            for c in range(TILES):
                nc.tensor.transpose(turned[:, c, :], pos_g[g][:, c * P : (c + 1) * P], ident[:])
            col = sbuf(f"pos_col{g}", [P, TILES], F32)
            nc.scalar.copy(out=col[:], in_=turned[:, :, ROW])
            pos_col.append(col)
        for g in range(PASSES):
            spread = bank(f"pos_spread{g}", f"pb{g}", [P, KP])
            for c in range(TILES):
                nc.tensor.transpose(spread[:, c * P : (c + 1) * P], pos_col[g][:, c : c + 1].to_broadcast([P, P]), ident[:])
            nc.scalar.activation(
                out=ahead[:, g * KP : (g + 1) * KP], in_=spread[:], func=ACT.Relu, bias=q_bias[:], scale=PLACE_SCALE
            )

        q_bf = sbuf("q_bf", [P, NQ, PACK], BF16)
        nc.scalar.copy(out=q_bf[:], in_=q_raw[:].rearrange("p j w -> p w j"))
        q_codes = sbuf("q_codes", [P, NQ], U32)
        q_scales = sbuf("q_scales", [P, NQ], U8)
        nc.vector.quantize_mx(out=q_codes[:].bitcast(FP8X4), scales=q_scales[:], in_=q_bf[:].rearrange("p w j -> p (w j)"))

        ks_g = sbuf("ks_g", [P, N], U8, tag="pos_pool")
        nc.vector.tensor_copy(out=ks_g[:], in_=ks_pool[:].indirect(offsets[:]))
        neg = sbuf("neg", [P, N], F32)
        kw_g = [sbuf("kw_g0", [P, KP], U32, tag="ks_pool"), sbuf("kw_g1", [P, KP], U32)]
        scores = [bank(f"scores{g}", f"pt{PASSES - 1 - g}", [P, KP]) for g in range(PASSES)]
        for g in range(PASSES):
            nc.vector.tensor_copy(out=kw_g[g][:], in_=kw_pool[:].bitcast(U32).indirect(listed(g)))
            nc.tensor.matmul_mx(
                out=scores[g][:],
                lhsT=q_codes[:].bitcast(FP8X4),
                lhsT_scale=q_scales[:],
                rhs=kw_g[g][:].bitcast(FP8X4),
                rhs_scale=ks_g[:, g * KP : (g + 1) * KP],
                start=True,
                stop=True,
            )
        for g in range(PASSES):
            cols = slice(g * KP, (g + 1) * KP)
            nc.vector.scalar_tensor_tensor(
                out=neg[:, cols], in0=ahead[:, cols], scalar=MASKED, in1=scores[g][:], op0=ALU.min, op1=ALU.subtract
            )
        neg_max = sbuf("neg_max", [P, 1], F32)
        nc.vector.tensor_reduce(out=neg_max[:], in_=neg[:], axis=mybir.AxisListType.X, op=ALU.min)

        v_pool = sbuf("v_pool", [P, T, 2], BF16)
        for c in range(V_CHUNKS):
            nc.scalar.activation(
                out=v_pool[:, c * V_CHUNK : (c + 1) * V_CHUNK, :], in_=v_raw[c][:].rearrange("p j t -> p t j"), func=ACT.Copy
            )


        part_sum = [sbuf(f"part_sum{g}", [P, 1], F32) for g in range(PASSES)]
        probs = []
        for g in range(PASSES):
            prob = sbuf(f"prob{g}", [P, KP], F32, tag=f"v_raw{V_CHUNKS - 1}" if g == 0 else "")
            nc.scalar.activation(
                out=prob[:],
                in_=neg[:, g * KP : (g + 1) * KP],
                func=ACT.Exp,
                bias=neg_max[:],
                scale=-1.0,
                accum_out=part_sum[g][:],
            )
            probs.append(prob)

        v_words = v_pool[:].rearrange("p t j -> p (t j)").bitcast(U32)
        v_bf = []
        for g in range(PASSES):
            v_dealt = sbuf(f"v_dealt{g}", [P, 2, BLOCKS, HALF], U32, tag="ahead" if g == 0 else "")
            nc.vector.tensor_copy(out=v_dealt[:].rearrange("p u b k -> p b u k"), in_=v_words.indirect(listed(g)))
            turned = bank(f"v_turned{g}", f"pt{g}", [P, PACK, P])
            for u in range(2):
                half = v_dealt[:, u, :, :].rearrange("p b k -> p (b k)").bitcast(F32)
                for e in range(2):
                    nc.tensor.transpose(turned[:, 2 * u + e, :], half[:, e : 2 * P : 2], ident[:])
            woven = sbuf(f"v_bf{g}", [P, DV, PACK], BF16)
            nc.scalar.copy(out=woven[:], in_=turned[:].bitcast(BF16).rearrange("p t e -> p e t"))
            v_bf.append(woven)

        vs_g = sbuf("vs_g", [P, N], F32, tag="v_pool")
        nc.vector.tensor_copy(out=vs_g[:], in_=vs_pool[:].indirect(offsets[:]))
        w_codes, w_scales = [], []
        w_dealt = []
        for g in range(PASSES):
            dealt = sbuf(f"w_dealt{g}", [P, 2, BLOCKS, HALF], BF16)
            nc.vector.tensor_tensor(
                out=dealt[:].rearrange("p u b k -> p b u k"),
                in0=probs[g][:].rearrange("p (b u k) -> p b u k", u=2, k=HALF),
                in1=vs_g[:, g * KP : (g + 1) * KP].rearrange("p (b u k) -> p b u k", u=2, k=HALF),
                op=ALU.mult,
            )
            w_dealt.append(dealt)
        w_bf = []
        for g in range(PASSES):
            turned = bank(f"w_turned{g}", f"pt{g}", [P, 2, NQ])
            for u in range(2):
                nc.tensor.transpose(turned[:, u, :], w_dealt[g][:, u, :, :].rearrange("p b k -> p (b k)").bitcast(F32), ident[:])
            woven = sbuf(f"w_bf{g}", [P, NQ, PACK], BF16)
            nc.scalar.copy(
                out=woven[:].rearrange("p q t -> p (q t)").bitcast(F32).rearrange("p (q u) -> p q u", u=2),
                in_=turned[:].rearrange("p u q -> p q u"),
            )
            w_bf.append(woven)
        for g in range(PASSES):
            codes = sbuf(f"w_codes{g}", [P, NQ], U32)
            scales = sbuf(f"w_scales{g}", [P, NQ], U8)
            nc.vector.quantize_mx(out=codes[:].bitcast(FP8X4), scales=scales[:], in_=w_bf[g][:].rearrange("p q t -> p (q t)"))
            w_codes.append(codes)
            w_scales.append(scales)
        total = sbuf("total", [P, 1], F32)
        nc.gpsimd.tensor_tensor(out=total[:], in0=part_sum[0][:], in1=part_sum[1][:], op=ALU.add)
        inv_total = sbuf("inv_total", [P, 1], F32)
        nc.vector.reciprocal(out=inv_total[:], in_=total[:])

        acc = bank("acc", "acc", [P, DV])
        for g in range(PASSES):
            codes = sbuf(f"v_codes{g}", [P, DV], U32)
            scales = sbuf(f"v_scales{g}", [P, DV], U8)
            nc.vector.quantize_mx(out=codes[:].bitcast(FP8X4), scales=scales[:], in_=v_bf[g][:].rearrange("p e t -> p (e t)"))
            nc.tensor.matmul_mx(
                out=acc[:],
                lhsT=w_codes[g][:].bitcast(FP8X4),
                lhsT_scale=w_scales[g][:],
                rhs=codes[:].bitcast(FP8X4),
                rhs_scale=scales[:],
                start=(g == 0),
                stop=(g == PASSES - 1),
            )
        result = sbuf("result", [P, DV], F32)
        nc.vector.tensor_scalar(out=result[:], in0=acc[:], scalar1=inv_total[:], scalar2=None, op0=ALU.mult)
        nc.sync.dma_start(out=out[0], in_=result[:])
